import numpy as np
import ml_dtypes


def mxq(x, axis, fmt="e4m3"):
    dtype, down = {"e4m3": (ml_dtypes.float8_e4m3fn, 7), "e5m2": (ml_dtypes.float8_e5m2, 14)}[fmt]
    v = np.moveaxis(np.asarray(x, np.float32).astype(ml_dtypes.bfloat16).astype(np.float64), axis, -1)
    blocks = v.reshape(v.shape[:-1] + (-1, 32))
    amax = np.abs(blocks).max(-1, keepdims=True)
    byte = np.maximum(np.where(amax > 0, np.frexp(amax)[1] - 1 + 127, 0) - down, 1)
    scale = np.exp2(byte - 127.0)
    codes = (blocks / scale).astype(np.float32).astype(dtype).astype(np.float64)
    return np.moveaxis((codes * scale).reshape(v.shape), -1, axis)


WIDE = False


def mx_kscale(k):
    if not WIDE:
        return np.ones(k)
    levels = np.array([10, -10, 5, -5, 0])
    if k % 512:
        return np.exp2(np.random.permutation(np.resize(levels, k // 32))).repeat(32)
    a = np.empty((k // 512, 16))
    for p in range(k // 512):
        a[p, :8] = np.random.permutation(np.resize(levels, 8))
        for g in range(8):
            far = levels[np.abs(levels - a[p, g]) >= 10]
            a[p, g + 8] = far[np.random.randint(len(far))]
    return np.exp2(a.ravel()).repeat(32)


def f64(x):
    return np.asarray(x).astype(np.float64)


def striped(idx):
    return np.tile(idx.reshape(-1, 16).T, (8, 1)).astype(np.uint16)


def unstriped(offs):
    return offs[:16].T.reshape(-1).astype(np.int64)


def pack_weight(w):
    k, n = w.shape
    w = f64(np.asarray(w, np.float32).astype(ml_dtypes.bfloat16)).reshape(k // 32, 32, n)
    amax = np.abs(w).max(1)
    byte = np.clip(np.where(amax > 0, np.frexp(amax)[1] - 1 + 127 - 7, 1), 1, 254)
    scaled = (w * np.exp2(127.0 - byte)[:, None, :]).reshape(k, n).astype(np.float32)
    words = np.ascontiguousarray(scaled.reshape(k // 512, 128, 4, n).transpose(0, 1, 3, 2)).astype(ml_dtypes.float8_e4m3fn).view(np.uint8)
    return words, np.ascontiguousarray(byte.astype(np.uint8).reshape(k // 512, 16, n))


def unpack_weight(words, scales):
    g, p, n, _ = words.shape
    vals = np.ascontiguousarray(words).view(ml_dtypes.float8_e4m3fn).astype(np.float64) * np.repeat(np.exp2(scales.astype(np.float64) - 127.0), 8, axis=1)[..., None]
    return vals.transpose(0, 1, 3, 2).reshape(g * 512, n)


E2M1 = np.array([0.0, 0.5, 1.0, 1.5, 2.0, 3.0, 4.0, 6.0, -0.0, -0.5, -1.0, -1.5, -2.0, -3.0, -4.0, -6.0])


def pack_fp4(w):
    k, n = w.shape
    w = f64(np.asarray(w, np.float32).astype(ml_dtypes.bfloat16)).reshape(k // 32, 32, n)
    amax = np.abs(w).max(1)
    mant, ex = np.frexp(amax / 6.0)
    byte = np.clip(np.where(amax > 0, np.where(mant > 0.5, ex, ex - 1) + 127, 1), 1, 254)
    scaled = (w * np.exp2(127.0 - byte)[:, None, :]).reshape(k, n).astype(np.float32)
    c = np.ascontiguousarray(scaled.reshape(k // 512, 128, 4, n).transpose(0, 1, 3, 2)).astype(ml_dtypes.float4_e2m1fn).view(np.uint8) & 0xF
    words = (c[..., 0::2] | (c[..., 1::2] << 4)).reshape(k // 512, 128, 2 * n)
    return np.ascontiguousarray(words), np.ascontiguousarray(byte.astype(np.uint8).reshape(k // 512, 16, n))


def unpack_fp4(words, scales):
    g, _, n = scales.shape
    words = np.ascontiguousarray(words).reshape(g, 128, n, 2)
    nib = np.empty((g, 128, n, 4), np.uint8)
    nib[..., 0::2] = words & 0xF
    nib[..., 1::2] = words >> 4
    vals = E2M1[nib] * np.repeat(np.exp2(scales.astype(np.float64) - 127.0), 8, axis=1)[..., None]
    return vals.transpose(0, 1, 3, 2).reshape(g * 512, n)


def planes(y):
    n, m = y.shape
    v = y.astype(np.float32).astype(ml_dtypes.bfloat16).astype(np.float64).reshape(n // 32, 32, m)
    top = np.abs(v).max(1)
    byte = np.clip(np.where(top > 0, np.frexp(top)[1] - 1 + 127 - 7, 1), 1, 254)
    codes = (v * np.exp2(127.0 - byte)[:, None, :]).reshape(n, m).astype(np.float32).astype(ml_dtypes.float8_e4m3fn).view(np.uint8)
    words = codes.reshape(n // 512, 128, 4, m).transpose(0, 1, 3, 2)
    return np.ascontiguousarray(words), np.ascontiguousarray(byte.astype(np.uint8).reshape(n // 512, 16, m))


K, T, S, N, H = 512, 1024, 512, 512, 512


def setup_inputs():
    n = np.random.standard_normal
    s = mx_kscale(K)[:, None]
    u = mx_kscale(H)
    packed_xT = pack_weight(n((K, T)) * s)
    packed_w1 = pack_fp4(n((K, N)) / np.sqrt(K) / s)
    packed_w2 = pack_fp4(n((H, N)) / np.sqrt(H) / u[:, None])
    return {
        "x_words": packed_xT[0],
        "x_scales": packed_xT[1],
        "w1_words": packed_w1[0],
        "w1_scales": packed_w1[1],
        "dir_": (np.random.uniform(0.1, 0.9, (H, S))).astype(np.float32),
        "unit": (np.random.uniform(0.6, 1.4, (H, 1)) * u[:, None]).astype(np.float32),
        "w2_words": packed_w2[0],
        "w2_scales": packed_w2[1],
        "offs": striped(np.random.permutation(T)[:S]),
        "c1": striped(np.random.permutation(S)),
        "c2": striped(np.random.permutation(S)),
    }


def reference(x_words, x_scales, w1_words, w1_scales, dir_, unit, w2_words, w2_scales, offs, c1, c2):
    xq = unpack_weight(x_words, x_scales)[:, unstriped(offs)]
    y = unpack_fp4(w1_words, w1_scales).T @ xq
    yp = y[:, unstriped(c1)]
    lo = np.minimum(y, yp)
    hi = np.maximum(y, yp)
    stg = f64(dir_) * lo + (-1.0 * f64(dir_) + 1.0) * hi
    mp = stg[:, unstriped(c2)]
    up2_ = np.maximum(stg, mp)
    lp = lo[:, unstriped(c2)]
    hid = f64(unit) * (up2_ - lp)
    out_0 = unpack_fp4(w2_words, w2_scales).T @ mxq(hid, 0, "e4m3")
    return (out_0,) + planes(out_0)

@@ -1,0 +1,255 @@
+from contextlib import ExitStack
+
+import concourse.mybir as mybir
+
+K, T, S, N, H = 512, 1024, 512, 512, 512
+FLOPS = 2 * K * H * S + 2 * H * N * S
+
+F32 = mybir.dt.float32
+BF16 = mybir.dt.bfloat16
+I32 = mybir.dt.int32
+U32 = mybir.dt.uint32
+U16 = mybir.dt.uint16
+U8 = mybir.dt.uint8
+FP8X4 = mybir.dt.float8_e4m3fn_x4
+FP4X4 = mybir.dt.float4_e2m1fn_x4
+ALU = mybir.AluOpType
+ACT = mybir.ActivationFunctionType
+
+P = 128
+PACK = 4
+HALF = S // 2
+CHUNKS = (256, 128, 128)
+LO_ON_SCALAR = {(i, t) for i in range(3) for t in range(3)}
+MP_PLACE = (0, 2, 0)
+LP_PLACE = (2, 3, 1)
+
+
+def load_scale_rows(queue, plane, rows):
+    for q in range(4):
+        queue.dma_start(out=plane[32 * q : 32 * q + 4, :].bitcast(I32), in_=rows[4 * q : 4 * q + 4, :].bitcast(I32))
+
+
+def deal_words(nc, words, raw_words, t0, t1):
+    nc.vector.tensor_copy(
+        out=words[:].rearrange("p (t m b) -> p t m b", t=PACK, b=2)[:, t0:t1],
+        in_=raw_words[:].rearrange("p (m t b) -> p t m b", t=PACK, b=2)[:, t0:t1],
+    )
+
+
+def deal_scales(nc, scales, raw_scales):
+    nc.vector.tensor_copy(
+        out=scales[:].rearrange("p (t m) -> p t m", t=PACK),
+        in_=raw_scales[:].rearrange("p (m t) -> p t m", t=PACK),
+    )
+
+
+def entries(lst, start, count):
+    return lst[:, start // 16 : (start + count) // 16]
+
+
+def tile_picked_ybitonc_hard_po_kernel(
+    tc, x_words, x_scales, w1_words, w1_scales, dir_, unit, w2_words, w2_scales, offs, c1, c2, out_0, out_1, out_2
+):
+    nc = tc.nc
+    with ExitStack() as ctx:
+        keep = ctx.enter_context(tc.tile_pool(name="keep", bufs=1))
+        psum = ctx.enter_context(tc.psum_pool(name="psum", bufs=1))
+
+        offs_sb = keep.tile([P, S // 16], U16, name="offs_sb")
+        c1_sb = keep.tile([P, S // 16], U16, name="c1_sb")
+        c2_sb = keep.tile([P, S // 16], U16, name="c2_sb")
+        x_table = keep.tile([P, T], I32, name="x_table")
+        x_table_scales = keep.tile([P, T], U8, name="x_table_scales")
+        w1_raw = keep.tile([P, 2 * H], U8, name="w1_raw")
+        w1_raw_scales = keep.tile([P, H], U8, name="w1_raw_scales")
+        w2_raw = keep.tile([P, 2 * N], U8, name="w2_raw")
+        w2_raw_scales = keep.tile([P, N], U8, name="w2_raw_scales")
+        unit_sb = keep.tile([P, PACK], F32, name="unit_sb")
+        dir_sb = [keep.tile([P, 2, S], F32, name="dir_sb%d" % h) for h in range(2)]
+
+        nc.gpsimd.memset(x_table_scales[:].bitcast(I32), 0)
+        nc.gpsimd.memset(w1_raw_scales[:].bitcast(I32), 0)
+        nc.gpsimd.memset(w2_raw_scales[:].bitcast(I32), 0)
+
+        nc.sync.dma_start(offs_sb[:], offs)
+        load_scale_rows(nc.scalar, x_table_scales, x_scales[0])
+        nc.sync.dma_start(out=w1_raw[:].bitcast(I32), in_=w1_words[0].bitcast(I32))
+        nc.sync.dma_start(out=x_table[:], in_=x_words[0].rearrange("p n t -> p (n t)").bitcast(I32))
+        load_scale_rows(nc.sync, w1_raw_scales, w1_scales[0])
+        nc.sync.dma_start(c1_sb[:], c1)
+        nc.sync.dma_start(out=w2_raw[:].bitcast(I32), in_=w2_words[0].bitcast(I32))
+        load_scale_rows(nc.sync, w2_raw_scales, w2_scales[0])
+        dir_rows = dir_.rearrange("(p t) j -> p t j", t=PACK)
+        for h in range(2):
+            nc.sync.dma_start(out=dir_sb[h][:], in_=dir_rows[:, 2 * h : 2 * h + 2, :])
+        nc.sync.dma_start(c2_sb[:], c2)
+        nc.sync.dma_start(out=unit_sb[:], in_=unit.rearrange("(p t) o -> p (t o)", t=PACK))
+
+        x_codes = keep.tile([P, S], U32, name="x_codes", align_bytes=64)
+        x_bytes = keep.tile([P, S], U8, name="x_bytes", align_bytes=64)
+        w1_dealt = keep.tile([P, 2 * H], U8, name="w1_dealt", align_bytes=64)
+        w1_dealt_scales = keep.tile([P, H], U8, name="w1_dealt_scales", align_bytes=64)
+        w2_dealt = keep.tile([P, 2 * N], U8, name="w2_dealt", align_bytes=64)
+        w2_dealt_scales = keep.tile([P, N], U8, name="w2_dealt_scales", align_bytes=64)
+
+        nc.vector.tensor_copy(x_bytes[:], x_table_scales[:].indirect(offs_sb[:]))
+        deal_words(nc, w1_dealt, w1_raw, 0, 1)
+        nc.vector.tensor_copy(x_codes[:], x_table[:].bitcast(U32).indirect(offs_sb[:]))
+        deal_scales(nc, w1_dealt_scales, w1_raw_scales)
+        deal_words(nc, w1_dealt, w1_raw, 1, PACK)
+
+        minus_unit = keep.tile([P, PACK], F32, name="minus_unit")
+        nc.gpsimd.tensor_scalar(minus_unit[:], unit_sb[:], -1.0, 0.0, ALU.mult, ALU.add)
+
+        y, yp, lo, stg, diff, gap, lift = [], [], [], [], [], [], []
+        for t in range(PACK):
+            for name, lst in (("y", y), ("yp", yp), ("lo", lo), ("stg", stg), ("diff", diff), ("gap", gap), ("lift", lift)):
+                lst.append(keep.tile([P, S], F32, name="%s%d" % (name, t)))
+
+        def front(t):
+            acc = psum.tile([P, S], F32, name="y_acc%d" % t)
+            nc.tensor.matmul_mx(
+                out=acc[:],
+                lhsT=w1_dealt[:, 2 * P * t : 2 * P * (t + 1)].bitcast(FP4X4),
+                lhsT_scale=w1_dealt_scales[:, P * t : P * (t + 1)],
+                rhs=x_codes[:].bitcast(FP8X4),
+                rhs_scale=x_bytes[:],
+                start=True,
+                stop=True,
+            )
+            nc.scalar.copy(y[t][:], acc[:])
+            for j0 in (0, HALF):
+                partners = y[t][:].indirect(entries(c1_sb, j0, HALF))
+                if (t, j0) in {(0, 0), (0, HALF)}:
+                    nc.vector.tensor_copy(yp[t][:, j0 : j0 + HALF], partners)
+                else:
+                    nc.scalar.activation(yp[t][:, j0 : j0 + HALF], partners, ACT.Copy)
+
+        def middle(t):
+            nc.vector.tensor_tensor(diff[t][:], yp[t][:], y[t][:], ALU.subtract)
+            nc.vector.tensor_tensor(lo[t][:], yp[t][:], y[t][:], ALU.min)
+            nc.scalar.activation(gap[t][:], diff[t][:], ACT.Abs)
+
+        def back(t):
+            nc.vector.scalar_tensor_tensor(lift[t][:], dir_sb[t // 2][:, t % 2, :], 1.0, gap[t][:], ALU.subtract, ALU.mult)
+
+        def last(t):
+            nc.vector.tensor_tensor(stg[t][:], lo[t][:], lift[t][:], ALU.subtract)
+
+        for step in range(PACK + 2):
+            if step < PACK:
+                front(step)
+            if 0 <= step - 2 < PACK:
+                back(step - 2)
+            if 0 <= step - 1 < PACK:
+                middle(step - 1)
+            if 0 <= step - 2 < PACK:
+                last(step - 2)
+            if step == 1:
+                deal_words(nc, w2_dealt, w2_raw, 0, PACK)
+                deal_scales(nc, w2_dealt_scales, w2_raw_scales)
+
+        out_codes = keep.tile([P, S], U32, name="out_codes", align_bytes=64)
+        out_bytes = keep.tile([P, S], U8, name="out_bytes", align_bytes=64)
+        out_rows = out_0.rearrange("(p t) j -> p t j", t=PACK)
+        out_words = out_1[0].rearrange("p n t -> p (n t)").bitcast(I32)
+
+        count = len(CHUNKS)
+        starts = [sum(CHUNKS[:i]) for i in range(count)]
+        mp, lp, up, fall, hid, rounded = {}, {}, {}, {}, {}, {}
+
+        scratch = [diff[2], diff[3], yp[3], gap[2]]
+
+        def look_up(i):
+            j0, w = starts[i], CHUNKS[i]
+            picks = entries(c2_sb, j0, w)
+            for t in range(PACK):
+                quarter = MP_PLACE[i] * P
+                mp[i, t] = scratch[t][:, quarter : quarter + w]
+                nc.scalar.activation(mp[i, t], stg[t][:].indirect(picks), ACT.Copy)
+                if (i, t) in LO_ON_SCALAR:
+                    quarter = LP_PLACE[i] * P
+                    lp[i, t] = scratch[t][:, quarter : quarter + w]
+                    nc.scalar.activation(lp[i, t], lo[t][:].indirect(picks), ACT.Copy)
+
+        def upper(i, t):
+            j0, w = starts[i], CHUNKS[i]
+            up[i, t] = keep.tile([P, w], F32, name="up%d_%d" % (i, t))
+            nc.vector.tensor_tensor(up[i, t][:], stg[t][:, j0 : j0 + w], mp[i, t], ALU.max)
+
+        def lower(i, t):
+            j0, w = starts[i], CHUNKS[i]
+            if t == 0:
+                fall[i] = keep.tile([P, PACK, w], F32, name="fall%d" % i)
+            if (i, t) in LO_ON_SCALAR:
+                partner_lo = lp[i, t]
+            else:
+                partner_lo = lo[t][:].indirect(entries(c2_sb, j0, w))
+            nc.vector.tensor_tensor(fall[i][:, t, :], partner_lo, up[i, t][:], ALU.subtract)
+
+        def round_hid(i):
+            w = CHUNKS[i]
+            hid[i] = keep.tile([P, w * PACK], BF16, name="hid%d" % i, align_bytes=64)
+            nc.vector.tensor_tensor(
+                hid[i][:].rearrange("p (c i t) -> p c t i", i=4, t=PACK),
+                fall[i][:].rearrange("p t (c i) -> p c t i", i=4),
+                minus_unit[:].unsqueeze(1).unsqueeze(3).to_broadcast([P, w // 4, PACK, 4]),
+                ALU.mult,
+            )
+
+        def product(i):
+            j0, w = starts[i], CHUNKS[i]
+            hid_codes = keep.tile([P, w], U32, name="hid_codes%d" % i, align_bytes=64)
+            hid_bytes = keep.tile([P, w], U8, name="hid_bytes%d" % i, align_bytes=64)
+            nc.vector.quantize_mx(out=hid_codes[:].bitcast(FP8X4), scales=hid_bytes[:], in_=hid[i][:])
+            result = keep.tile([P, PACK, w], F32, name="result%d" % i)
+            rounded[i] = keep.tile([P, w * PACK], BF16, name="rounded%d" % i, align_bytes=64)
+            for b in range(w // P):
+                acc = psum.tile([P, PACK, P], F32, name="out_acc%d" % (j0 // P + b))
+                for t in range(PACK):
+                    nc.tensor.matmul_mx(
+                        out=acc[:, t, :],
+                        lhsT=w2_dealt[:, 2 * P * t : 2 * P * (t + 1)].bitcast(FP4X4),
+                        lhsT_scale=w2_dealt_scales[:, P * t : P * (t + 1)],
+                        rhs=hid_codes[:, P * b : P * (b + 1)].bitcast(FP8X4),
+                        rhs_scale=hid_bytes[:, P * b : P * (b + 1)],
+                        start=True,
+                        stop=True,
+                    )
+                nc.scalar.copy(
+                    rounded[i][:, PACK * P * b : PACK * P * (b + 1)].rearrange("p (c t) -> p c t", t=PACK),
+                    acc[:].rearrange("p t c -> p c t"),
+                )
+                nc.scalar.copy(result[:, :, P * b : P * (b + 1)], acc[:])
+            nc.sync.dma_start(out=out_rows[:, :, j0 : j0 + w], in_=result[:])
+
+        def planes(i):
+            j0, w = starts[i], CHUNKS[i]
+            nc.vector.quantize_mx(
+                out=out_codes[:, j0 : j0 + w].bitcast(FP8X4), scales=out_bytes[:, j0 : j0 + w], in_=rounded[i][:]
+            )
+            nc.sync.dma_start(out=out_words[:, j0 : j0 + w], in_=out_codes[:, j0 : j0 + w].bitcast(I32))
+
+        look_up(0)
+        for i in range(count):
+            upper(i, 0)
+            if i >= 1:
+                product(i - 1)
+            for t in range(1, PACK):
+                upper(i, t)
+                lower(i, t - 1)
+            lower(i, PACK - 1)
+            if i + 1 < count:
+                look_up(i + 1)
+            if i >= 2:
+                planes(i - 2)
+            round_hid(i)
+        planes(count - 2)
+        product(count - 1)
+        planes(count - 1)
+        for q in range(4):
+            queue = nc.sync if q % 2 == 0 else nc.scalar
+            queue.dma_start(
+                out=out_2[0, 4 * q : 4 * q + 4, :].bitcast(I32), in_=out_bytes[32 * q : 32 * q + 4, :].bitcast(I32)
+            )

@@ -19,28 +19,27 @@ ACT = mybir.ActivationFunctionType
 P = 128
 PACK = 4
 HALF = S // 2
+SPARE = 16
 CHUNKS = (256, 128, 128)
-LO_ON_SCALAR = {(i, t) for i in range(3) for t in range(3)}
-MP_PLACE = (0, 2, 0)
-LP_PLACE = (2, 3, 1)
+LO_ON_SCALAR = (2, 2)
 
 
-def load_scale_rows(queue, plane, rows):
-    for q in range(4):
+def load_scale_rows(queues, plane, rows):
+    for q, queue in enumerate(queues):
         queue.dma_start(out=plane[32 * q : 32 * q + 4, :].bitcast(I32), in_=rows[4 * q : 4 * q + 4, :].bitcast(I32))
 
 
 def deal_words(nc, words, raw_words, t0, t1):
     nc.vector.tensor_copy(
-        out=words[:].rearrange("p (t m b) -> p t m b", t=PACK, b=2)[:, t0:t1],
-        in_=raw_words[:].rearrange("p (m t b) -> p t m b", t=PACK, b=2)[:, t0:t1],
+        out=words[:].bitcast(U16).rearrange("p (t m) -> p t m", t=t1 - t0),
+        in_=raw_words[:].bitcast(U16).rearrange("p (m t) -> p t m", t=PACK)[:, t0:t1],
     )
 
 
-def deal_scales(nc, scales, raw_scales):
+def deal_scales(nc, scales, raw_scales, t0, t1):
     nc.vector.tensor_copy(
-        out=scales[:].rearrange("p (t m) -> p t m", t=PACK),
-        in_=raw_scales[:].rearrange("p (m t) -> p t m", t=PACK),
+        out=scales[:].rearrange("p (t m) -> p t m", t=PACK)[:, t0:t1],
+        in_=raw_scales[:].rearrange("p (m t) -> p t m", t=PACK)[:, t0:t1],
     )
 
 
@@ -62,7 +61,7 @@ def tile_picked_ybitonc_hard_po_kernel(
         x_table = keep.tile([P, T], I32, name="x_table")
         x_table_scales = keep.tile([P, T], U8, name="x_table_scales")
         w1_raw = keep.tile([P, 2 * H], U8, name="w1_raw")
-        w1_raw_scales = keep.tile([P, H], U8, name="w1_raw_scales")
+        w1_raw_scales = keep.tile([P, H], U8, name="w1_raw_scales", tag="w1_reused", align_bytes=64)
         w2_raw = keep.tile([P, 2 * N], U8, name="w2_raw")
         w2_raw_scales = keep.tile([P, N], U8, name="w2_raw_scales")
         unit_sb = keep.tile([P, PACK], F32, name="unit_sb")
@@ -73,69 +72,87 @@ def tile_picked_ybitonc_hard_po_kernel(
         nc.gpsimd.memset(w2_raw_scales[:].bitcast(I32), 0)
 
         nc.sync.dma_start(offs_sb[:], offs)
-        load_scale_rows(nc.scalar, x_table_scales, x_scales[0])
-        nc.sync.dma_start(out=w1_raw[:].bitcast(I32), in_=w1_words[0].bitcast(I32))
+        load_scale_rows((nc.scalar, nc.sync, nc.scalar, nc.sync), x_table_scales, x_scales[0])
         nc.sync.dma_start(out=x_table[:], in_=x_words[0].rearrange("p n t -> p (n t)").bitcast(I32))
-        load_scale_rows(nc.sync, w1_raw_scales, w1_scales[0])
+        nc.scalar.dma_start(out=w1_raw[:].bitcast(I32), in_=w1_words[0].bitcast(I32))
+        load_scale_rows((nc.scalar, nc.sync, nc.sync, nc.sync), w1_raw_scales, w1_scales[0])
         nc.sync.dma_start(c1_sb[:], c1)
-        nc.sync.dma_start(out=w2_raw[:].bitcast(I32), in_=w2_words[0].bitcast(I32))
-        load_scale_rows(nc.sync, w2_raw_scales, w2_scales[0])
         dir_rows = dir_.rearrange("(p t) j -> p t j", t=PACK)
-        for h in range(2):
-            nc.sync.dma_start(out=dir_sb[h][:], in_=dir_rows[:, 2 * h : 2 * h + 2, :])
+        nc.sync.dma_start(out=dir_sb[0][:], in_=dir_rows[:, 0:2, :])
+        load_scale_rows((nc.sync,) * 4, w2_raw_scales, w2_scales[0])
+        nc.sync.dma_start(out=w2_raw[:].bitcast(I32), in_=w2_words[0].bitcast(I32))
+        nc.sync.dma_start(out=dir_sb[1][:], in_=dir_rows[:, 2:4, :])
         nc.sync.dma_start(c2_sb[:], c2)
         nc.sync.dma_start(out=unit_sb[:], in_=unit.rearrange("(p t) o -> p (t o)", t=PACK))
 
         x_codes = keep.tile([P, S], U32, name="x_codes", align_bytes=64)
         x_bytes = keep.tile([P, S], U8, name="x_bytes", align_bytes=64)
-        w1_dealt = keep.tile([P, 2 * H], U8, name="w1_dealt", align_bytes=64)
+        w1_first = keep.tile([P, 2 * P], U8, name="w1_first", align_bytes=64)
         w1_dealt_scales = keep.tile([P, H], U8, name="w1_dealt_scales", align_bytes=64)
         w2_dealt = keep.tile([P, 2 * N], U8, name="w2_dealt", align_bytes=64)
         w2_dealt_scales = keep.tile([P, N], U8, name="w2_dealt_scales", align_bytes=64)
 
         nc.vector.tensor_copy(x_bytes[:], x_table_scales[:].indirect(offs_sb[:]))
-        deal_words(nc, w1_dealt, w1_raw, 0, 1)
+        deal_words(nc, w1_first, w1_raw, 0, 1)
         nc.vector.tensor_copy(x_codes[:], x_table[:].bitcast(U32).indirect(offs_sb[:]))
-        deal_scales(nc, w1_dealt_scales, w1_raw_scales)
-        deal_words(nc, w1_dealt, w1_raw, 1, PACK)
+        deal_scales(nc, w1_dealt_scales, w1_raw_scales, 0, PACK)
+        w1_rest = keep.tile([P, 2 * P * (PACK - 1)], U8, name="w1_rest", tag="w1_reused", align_bytes=64)
+        deal_words(nc, w1_rest, w1_raw, 1, PACK)
+        w1_tiles = [w1_first[:]] + [w1_rest[:, 2 * P * t : 2 * P * (t + 1)] for t in range(PACK - 1)]
 
         minus_unit = keep.tile([P, PACK], F32, name="minus_unit")
         nc.gpsimd.tensor_scalar(minus_unit[:], unit_sb[:], -1.0, 0.0, ALU.mult, ALU.add)
 
-        y, yp, lo, stg, diff, gap, lift = [], [], [], [], [], [], []
-        for t in range(PACK):
-            for name, lst in (("y", y), ("yp", yp), ("lo", lo), ("stg", stg), ("diff", diff), ("gap", gap), ("lift", lift)):
-                lst.append(keep.tile([P, S], F32, name="%s%d" % (name, t)))
+        def rows(name, count):
+            return [keep.tile([P, S], F32, name="%s%d" % (name, t))[:] for t in range(count)]
+
+        scratch = keep.tile([P, PACK, S], F32, name="scratch")
+        stg = keep.tile([P, PACK, S], F32, name="stg")
+        yp, lo = rows("yp", PACK), rows("lo", PACK)
+        y_wide = [keep.tile([P, S + SPARE], F32, name="y%d" % t) for t in range(PACK)]
+        y = [tile[:, :S] for tile in y_wide]
+        for tile in y_wide:
+            nc.gpsimd.memset(tile[:, S:], 0.0)
+        diff = rows("diff", 2) + [scratch[:, 0, :], scratch[:, 1, :]]
+        gap = rows("gap", 3) + [scratch[:, 2, :]]
+        lift = rows("lift", 3) + [scratch[:, 3, :]]
+        y_acc = {}
 
         def front(t):
-            acc = psum.tile([P, S], F32, name="y_acc%d" % t)
+            acc = y_acc[t] = psum.tile([P, S], F32, name="y_acc", tag="bank%d" % (t % 2))
             nc.tensor.matmul_mx(
                 out=acc[:],
-                lhsT=w1_dealt[:, 2 * P * t : 2 * P * (t + 1)].bitcast(FP4X4),
+                lhsT=w1_tiles[t].bitcast(FP4X4),
                 lhsT_scale=w1_dealt_scales[:, P * t : P * (t + 1)],
                 rhs=x_codes[:].bitcast(FP8X4),
                 rhs_scale=x_bytes[:],
                 start=True,
                 stop=True,
             )
-            nc.scalar.copy(y[t][:], acc[:])
+            nc.scalar.copy(y[t], acc[:])
+            if t >= 1:
+                nc.scalar.activation(yp[t], y_wide[t][:].indirect(c1_sb[:]), ACT.Copy)
+                return
             for j0 in (0, HALF):
-                partners = y[t][:].indirect(entries(c1_sb, j0, HALF))
-                if (t, j0) in {(0, 0), (0, HALF)}:
+                partners = y_wide[t][:].indirect(entries(c1_sb, j0, HALF))
+                if (t, j0) in {(0, HALF)}:
                     nc.vector.tensor_copy(yp[t][:, j0 : j0 + HALF], partners)
                 else:
                     nc.scalar.activation(yp[t][:, j0 : j0 + HALF], partners, ACT.Copy)
 
         def middle(t):
-            nc.vector.tensor_tensor(diff[t][:], yp[t][:], y[t][:], ALU.subtract)
-            nc.vector.tensor_tensor(lo[t][:], yp[t][:], y[t][:], ALU.min)
-            nc.scalar.activation(gap[t][:], diff[t][:], ACT.Abs)
+            nc.vector.tensor_tensor(diff[t], yp[t], y_acc[t][:], ALU.subtract)
+            nc.vector.tensor_tensor(lo[t], yp[t], y[t], ALU.min)
+            if t in ():
+                nc.vector.scalar_tensor_tensor(gap[t], diff[t], -1.0, diff[t], ALU.mult, ALU.max)
+            else:
+                nc.scalar.activation(gap[t], diff[t], ACT.Abs)
 
         def back(t):
-            nc.vector.scalar_tensor_tensor(lift[t][:], dir_sb[t // 2][:, t % 2, :], 1.0, gap[t][:], ALU.subtract, ALU.mult)
+            nc.vector.scalar_tensor_tensor(lift[t], dir_sb[t // 2][:, t % 2, :], 1.0, gap[t], ALU.subtract, ALU.mult)
 
         def last(t):
-            nc.vector.tensor_tensor(stg[t][:], lo[t][:], lift[t][:], ALU.subtract)
+            nc.vector.tensor_tensor(stg[:, t, :], lo[t], lift[t], ALU.subtract)
 
         for step in range(PACK + 2):
             if step < PACK:
@@ -148,7 +165,7 @@ def tile_picked_ybitonc_hard_po_kernel(
                 last(step - 2)
             if step == 1:
                 deal_words(nc, w2_dealt, w2_raw, 0, PACK)
-                deal_scales(nc, w2_dealt_scales, w2_raw_scales)
+                deal_scales(nc, w2_dealt_scales, w2_raw_scales, 0, PACK)
 
         out_codes = keep.tile([P, S], U32, name="out_codes", align_bytes=64)
         out_bytes = keep.tile([P, S], U8, name="out_bytes", align_bytes=64)
@@ -157,46 +174,52 @@ def tile_picked_ybitonc_hard_po_kernel(
 
         count = len(CHUNKS)
         starts = [sum(CHUNKS[:i]) for i in range(count)]
-        mp, lp, up, fall, hid, rounded = {}, {}, {}, {}, {}, {}
+        up, fall, hid, rounded = {}, {}, {}, {}
+        last_tile = PACK - 1
 
-        scratch = [diff[2], diff[3], yp[3], gap[2]]
+        def partner_stg(i):
+            return scratch[:, :, starts[i] % HALF : starts[i] % HALF + CHUNKS[i]]
 
-        def look_up(i):
-            j0, w = starts[i], CHUNKS[i]
-            picks = entries(c2_sb, j0, w)
+        def partner_lo(i):
+            return scratch[:, :, HALF + starts[i] % HALF : HALF + starts[i] % HALF + CHUNKS[i]]
+
+        def look_up(j0):
+            picks = entries(c2_sb, j0, HALF)
             for t in range(PACK):
-                quarter = MP_PLACE[i] * P
-                mp[i, t] = scratch[t][:, quarter : quarter + w]
-                nc.scalar.activation(mp[i, t], stg[t][:].indirect(picks), ACT.Copy)
-                if (i, t) in LO_ON_SCALAR:
-                    quarter = LP_PLACE[i] * P
-                    lp[i, t] = scratch[t][:, quarter : quarter + w]
-                    nc.scalar.activation(lp[i, t], lo[t][:].indirect(picks), ACT.Copy)
+                nc.scalar.activation(scratch[:, t, :HALF], stg[:, t, :].indirect(picks), ACT.Copy)
+            for t in range(LO_ON_SCALAR[j0 // HALF]):
+                nc.scalar.activation(scratch[:, t, HALF:], lo[t].indirect(picks), ACT.Copy)
 
-        def upper(i, t):
+        def upper(i, t0, t1):
             j0, w = starts[i], CHUNKS[i]
-            up[i, t] = keep.tile([P, w], F32, name="up%d_%d" % (i, t))
-            nc.vector.tensor_tensor(up[i, t][:], stg[t][:, j0 : j0 + w], mp[i, t], ALU.max)
+            nc.vector.tensor_tensor(up[i][:, t0:t1, :], stg[:, t0:t1, j0 : j0 + w], partner_stg(i)[:, t0:t1, :], ALU.max)
 
-        def lower(i, t):
-            j0, w = starts[i], CHUNKS[i]
-            if t == 0:
-                fall[i] = keep.tile([P, PACK, w], F32, name="fall%d" % i)
-            if (i, t) in LO_ON_SCALAR:
-                partner_lo = lp[i, t]
+        def lower(i):
+            n = LO_ON_SCALAR[starts[i] // HALF]
+            if n:
+                nc.vector.tensor_tensor(fall[i][:, :n, :], partner_lo(i)[:, :n, :], up[i][:, :n, :], ALU.subtract)
+            picks = entries(c2_sb, starts[i], CHUNKS[i])
+            for t in range(n, PACK):
+                nc.vector.tensor_tensor(fall[i][:, t, :], lo[t].indirect(picks), up[i][:, t, :], ALU.subtract)
+
+        def scale(i, t):
+            if (i, t) in ():
+                nc.scalar.activation(scaled[i][:, t, :], fall[i][:, t, :], ACT.Copy, scale=minus_unit[:, t : t + 1])
             else:
-                partner_lo = lo[t][:].indirect(entries(c2_sb, j0, w))
-            nc.vector.tensor_tensor(fall[i][:, t, :], partner_lo, up[i, t][:], ALU.subtract)
+                nc.vector.tensor_scalar(scaled[i][:, t, :], fall[i][:, t, :], minus_unit[:, t : t + 1], None, ALU.mult)
 
-        def round_hid(i):
-            w = CHUNKS[i]
-            hid[i] = keep.tile([P, w * PACK], BF16, name="hid%d" % i, align_bytes=64)
-            nc.vector.tensor_tensor(
+        def weave(i):
+            nc.vector.tensor_copy(
                 hid[i][:].rearrange("p (c i t) -> p c t i", i=4, t=PACK),
-                fall[i][:].rearrange("p t (c i) -> p c t i", i=4),
-                minus_unit[:].unsqueeze(1).unsqueeze(3).to_broadcast([P, w // 4, PACK, 4]),
-                ALU.mult,
+                scaled[i][:].rearrange("p t (c i) -> p c t i", i=4),
             )
+
+        scaled = {}
+        for i, w in enumerate(CHUNKS):
+            up[i] = keep.tile([P, PACK, w], F32, name="up%d" % i)
+            fall[i] = keep.tile([P, PACK, w], F32, name="fall%d" % i)
+            scaled[i] = keep.tile([P, PACK, w], BF16, name="scaled%d" % i)
+            hid[i] = keep.tile([P, w * PACK], BF16, name="hid%d" % i, align_bytes=64)
 
         def product(i):
             j0, w = starts[i], CHUNKS[i]
@@ -205,11 +228,13 @@ def tile_picked_ybitonc_hard_po_kernel(
             nc.vector.quantize_mx(out=hid_codes[:].bitcast(FP8X4), scales=hid_bytes[:], in_=hid[i][:])
             result = keep.tile([P, PACK, w], F32, name="result%d" % i)
             rounded[i] = keep.tile([P, w * PACK], BF16, name="rounded%d" % i, align_bytes=64)
+            final = i == count - 1
             for b in range(w // P):
                 acc = psum.tile([P, PACK, P], F32, name="out_acc%d" % (j0 // P + b))
+                other = psum.tile([P, PACK, P], F32, name="other", tag="bank0") if final else acc
                 for t in range(PACK):
                     nc.tensor.matmul_mx(
-                        out=acc[:, t, :],
+                        out=(acc if t < 2 else other)[:, t, :],
                         lhsT=w2_dealt[:, 2 * P * t : 2 * P * (t + 1)].bitcast(FP4X4),
                         lhsT_scale=w2_dealt_scales[:, P * t : P * (t + 1)],
                         rhs=hid_codes[:, P * b : P * (b + 1)].bitcast(FP8X4),
@@ -217,11 +242,19 @@ def tile_picked_ybitonc_hard_po_kernel(
                         start=True,
                         stop=True,
                     )
-                nc.scalar.copy(
-                    rounded[i][:, PACK * P * b : PACK * P * (b + 1)].rearrange("p (c t) -> p c t", t=PACK),
-                    acc[:].rearrange("p t c -> p c t"),
-                )
-                nc.scalar.copy(result[:, :, P * b : P * (b + 1)], acc[:])
+                if final:
+                    nc.scalar.copy(result[:, :2, :], acc[:, :2, :])
+                    nc.scalar.copy(result[:, 2:, :], other[:, 2:, :])
+                    nc.vector.tensor_copy(
+                        rounded[i][:].rearrange("p (c i t) -> p c t i", i=4, t=PACK),
+                        result[:].rearrange("p t (c i) -> p c t i", i=4),
+                    )
+                else:
+                    nc.scalar.copy(
+                        rounded[i][:, PACK * P * b : PACK * P * (b + 1)].rearrange("p (c t) -> p c t", t=PACK),
+                        acc[:].rearrange("p t c -> p c t"),
+                    )
+                    nc.scalar.copy(result[:, :, P * b : P * (b + 1)], acc[:])
             nc.sync.dma_start(out=out_rows[:, :, j0 : j0 + w], in_=result[:])
 
         def planes(i):
@@ -233,20 +266,20 @@ def tile_picked_ybitonc_hard_po_kernel(
 
         look_up(0)
         for i in range(count):
-            upper(i, 0)
+            upper(i, 0, 3)
             if i >= 1:
                 product(i - 1)
-            for t in range(1, PACK):
-                upper(i, t)
-                lower(i, t - 1)
-            lower(i, PACK - 1)
-            if i + 1 < count:
-                look_up(i + 1)
+            upper(i, 3, PACK)
+            lower(i)
+            if starts[i] + CHUNKS[i] == HALF:
+                look_up(HALF)
+            for t in range(PACK):
+                scale(i, t)
             if i >= 2:
                 planes(i - 2)
-            round_hid(i)
-        planes(count - 2)
+            weave(i)
         product(count - 1)
+        planes(count - 2)
         planes(count - 1)
         for q in range(4):
             queue = nc.sync if q % 2 == 0 else nc.scalar

@@ -21,7 +21,8 @@ PACK = 4
 HALF = S // 2
 SPARE = 16
 CHUNKS = (256, 128, 128)
-LO_ON_SCALAR = (2, 2)
+LO_ON_SCALAR = {(i, t) for i in range(2) for t in range(3)}
+OUT_BANKS = ("out0", "out1", "out2", "bank0_0", "bank0_256")
 
 
 def load_scale_rows(queues, plane, rows):
@@ -78,10 +79,10 @@ def tile_picked_ybitonc_hard_po_kernel(
         load_scale_rows((nc.scalar, nc.sync, nc.sync, nc.sync), w1_raw_scales, w1_scales[0])
         nc.sync.dma_start(c1_sb[:], c1)
         dir_rows = dir_.rearrange("(p t) j -> p t j", t=PACK)
-        nc.sync.dma_start(out=dir_sb[0][:], in_=dir_rows[:, 0:2, :])
         load_scale_rows((nc.sync,) * 4, w2_raw_scales, w2_scales[0])
         nc.sync.dma_start(out=w2_raw[:].bitcast(I32), in_=w2_words[0].bitcast(I32))
-        nc.sync.dma_start(out=dir_sb[1][:], in_=dir_rows[:, 2:4, :])
+        for h in range(2):
+            nc.sync.dma_start(out=dir_sb[h][:], in_=dir_rows[:, 2 * h : 2 * h + 2, :])
         nc.sync.dma_start(c2_sb[:], c2)
         nc.sync.dma_start(out=unit_sb[:], in_=unit.rearrange("(p t) o -> p (t o)", t=PACK))
 
@@ -94,8 +95,10 @@ def tile_picked_ybitonc_hard_po_kernel(
 
         nc.vector.tensor_copy(x_bytes[:], x_table_scales[:].indirect(offs_sb[:]))
         deal_words(nc, w1_first, w1_raw, 0, 1)
-        nc.vector.tensor_copy(x_codes[:], x_table[:].bitcast(U32).indirect(offs_sb[:]))
+        x_window = x_table[:].bitcast(U32)
+        nc.vector.tensor_copy(x_codes[:, :HALF], x_window.indirect(entries(offs_sb, 0, HALF)))
         deal_scales(nc, w1_dealt_scales, w1_raw_scales, 0, PACK)
+        nc.vector.tensor_copy(x_codes[:, HALF:], x_window.indirect(entries(offs_sb, HALF, HALF)))
         w1_rest = keep.tile([P, 2 * P * (PACK - 1)], U8, name="w1_rest", tag="w1_reused", align_bytes=64)
         deal_words(nc, w1_rest, w1_raw, 1, PACK)
         w1_tiles = [w1_first[:]] + [w1_rest[:, 2 * P * t : 2 * P * (t + 1)] for t in range(PACK - 1)]
@@ -106,53 +109,47 @@ def tile_picked_ybitonc_hard_po_kernel(
         def rows(name, count):
             return [keep.tile([P, S], F32, name="%s%d" % (name, t))[:] for t in range(count)]
 
-        scratch = keep.tile([P, PACK, S], F32, name="scratch")
-        stg = keep.tile([P, PACK, S], F32, name="stg")
-        yp, lo = rows("yp", PACK), rows("lo", PACK)
+        yp, lo, stg, diff, gap, lift = (rows(name, PACK) for name in ("yp", "lo", "stg", "diff", "gap", "lift"))
         y_wide = [keep.tile([P, S + SPARE], F32, name="y%d" % t) for t in range(PACK)]
         y = [tile[:, :S] for tile in y_wide]
         for tile in y_wide:
             nc.gpsimd.memset(tile[:, S:], 0.0)
-        diff = rows("diff", 2) + [scratch[:, 0, :], scratch[:, 1, :]]
-        gap = rows("gap", 3) + [scratch[:, 2, :]]
-        lift = rows("lift", 3) + [scratch[:, 3, :]]
-        y_acc = {}
 
         def front(t):
-            acc = y_acc[t] = psum.tile([P, S], F32, name="y_acc", tag="bank%d" % (t % 2))
-            nc.tensor.matmul_mx(
-                out=acc[:],
-                lhsT=w1_tiles[t].bitcast(FP4X4),
-                lhsT_scale=w1_dealt_scales[:, P * t : P * (t + 1)],
-                rhs=x_codes[:].bitcast(FP8X4),
-                rhs_scale=x_bytes[:],
-                start=True,
-                stop=True,
-            )
-            nc.scalar.copy(y[t], acc[:])
+            width = HALF if t == 0 else S
+            for j0 in range(0, S, width):
+                cols = slice(j0, j0 + width)
+                acc = psum.tile([P, width], F32, name="y_acc", tag="bank%d_%d" % (t, j0))
+                nc.tensor.matmul_mx(
+                    out=acc[:],
+                    lhsT=w1_tiles[t].bitcast(FP4X4),
+                    lhsT_scale=w1_dealt_scales[:, P * t : P * (t + 1)],
+                    rhs=x_codes[:, cols].bitcast(FP8X4),
+                    rhs_scale=x_bytes[:, cols],
+                    start=True,
+                    stop=True,
+                )
+                nc.scalar.copy(y[t][:, cols], acc[:])
             if t >= 1:
                 nc.scalar.activation(yp[t], y_wide[t][:].indirect(c1_sb[:]), ACT.Copy)
                 return
             for j0 in (0, HALF):
                 partners = y_wide[t][:].indirect(entries(c1_sb, j0, HALF))
-                if (t, j0) in {(0, HALF)}:
+                if (t, j0) in {(0, 0), (0, HALF)}:
                     nc.vector.tensor_copy(yp[t][:, j0 : j0 + HALF], partners)
                 else:
                     nc.scalar.activation(yp[t][:, j0 : j0 + HALF], partners, ACT.Copy)
 
         def middle(t):
-            nc.vector.tensor_tensor(diff[t], yp[t], y_acc[t][:], ALU.subtract)
+            nc.vector.tensor_tensor(diff[t], yp[t], y[t], ALU.subtract)
             nc.vector.tensor_tensor(lo[t], yp[t], y[t], ALU.min)
-            if t in ():
-                nc.vector.scalar_tensor_tensor(gap[t], diff[t], -1.0, diff[t], ALU.mult, ALU.max)
-            else:
-                nc.scalar.activation(gap[t], diff[t], ACT.Abs)
+            nc.scalar.activation(gap[t], diff[t], ACT.Abs)
 
         def back(t):
             nc.vector.scalar_tensor_tensor(lift[t], dir_sb[t // 2][:, t % 2, :], 1.0, gap[t], ALU.subtract, ALU.mult)
 
         def last(t):
-            nc.vector.tensor_tensor(stg[:, t, :], lo[t], lift[t], ALU.subtract)
+            nc.vector.tensor_tensor(stg[t], lo[t], lift[t], ALU.subtract)
 
         for step in range(PACK + 2):
             if step < PACK:
@@ -174,52 +171,41 @@ def tile_picked_ybitonc_hard_po_kernel(
 
         count = len(CHUNKS)
         starts = [sum(CHUNKS[:i]) for i in range(count)]
-        up, fall, hid, rounded = {}, {}, {}, {}
-        last_tile = PACK - 1
+        mp, lp, up, fall, hid, rounded = {}, {}, {}, {}, {}, {}
 
-        def partner_stg(i):
-            return scratch[:, :, starts[i] % HALF : starts[i] % HALF + CHUNKS[i]]
+        scratch = [diff[2], diff[3], yp[3], gap[2]]
 
-        def partner_lo(i):
-            return scratch[:, :, HALF + starts[i] % HALF : HALF + starts[i] % HALF + CHUNKS[i]]
-
-        def look_up(j0):
-            picks = entries(c2_sb, j0, HALF)
+        def look_up(half):
+            picks = entries(c2_sb, half * HALF, HALF)
             for t in range(PACK):
-                nc.scalar.activation(scratch[:, t, :HALF], stg[:, t, :].indirect(picks), ACT.Copy)
-            for t in range(LO_ON_SCALAR[j0 // HALF]):
-                nc.scalar.activation(scratch[:, t, HALF:], lo[t].indirect(picks), ACT.Copy)
+                nc.scalar.activation(scratch[t][:, :HALF], stg[t].indirect(picks), ACT.Copy)
+                if (half, t) in LO_ON_SCALAR:
+                    nc.scalar.activation(scratch[t][:, HALF:], lo[t].indirect(picks), ACT.Copy)
 
-        def upper(i, t0, t1):
+        def upper(i, t):
             j0, w = starts[i], CHUNKS[i]
-            nc.vector.tensor_tensor(up[i][:, t0:t1, :], stg[:, t0:t1, j0 : j0 + w], partner_stg(i)[:, t0:t1, :], ALU.max)
+            up[i, t] = keep.tile([P, w], F32, name="up%d_%d" % (i, t))
+            nc.vector.tensor_tensor(up[i, t][:], stg[t][:, j0 : j0 + w], scratch[t][:, j0 % HALF : j0 % HALF + w], ALU.max)
 
-        def lower(i):
-            n = LO_ON_SCALAR[starts[i] // HALF]
-            if n:
-                nc.vector.tensor_tensor(fall[i][:, :n, :], partner_lo(i)[:, :n, :], up[i][:, :n, :], ALU.subtract)
-            picks = entries(c2_sb, starts[i], CHUNKS[i])
-            for t in range(n, PACK):
-                nc.vector.tensor_tensor(fall[i][:, t, :], lo[t].indirect(picks), up[i][:, t, :], ALU.subtract)
-
-        def scale(i, t):
-            if (i, t) in ():
-                nc.scalar.activation(scaled[i][:, t, :], fall[i][:, t, :], ACT.Copy, scale=minus_unit[:, t : t + 1])
+        def lower(i, t):
+            j0, w = starts[i], CHUNKS[i]
+            if t == 0:
+                fall[i] = keep.tile([P, PACK, w], F32, name="fall%d" % i)
+            if (j0 // HALF, t) in LO_ON_SCALAR:
+                partner_lo = scratch[t][:, HALF + j0 % HALF : HALF + j0 % HALF + w]
             else:
-                nc.vector.tensor_scalar(scaled[i][:, t, :], fall[i][:, t, :], minus_unit[:, t : t + 1], None, ALU.mult)
+                partner_lo = lo[t].indirect(entries(c2_sb, j0, w))
+            nc.vector.tensor_tensor(fall[i][:, t, :], partner_lo, up[i, t][:], ALU.subtract)
 
-        def weave(i):
-            nc.vector.tensor_copy(
-                hid[i][:].rearrange("p (c i t) -> p c t i", i=4, t=PACK),
-                scaled[i][:].rearrange("p t (c i) -> p c t i", i=4),
-            )
-
-        scaled = {}
-        for i, w in enumerate(CHUNKS):
-            up[i] = keep.tile([P, PACK, w], F32, name="up%d" % i)
-            fall[i] = keep.tile([P, PACK, w], F32, name="fall%d" % i)
-            scaled[i] = keep.tile([P, PACK, w], BF16, name="scaled%d" % i)
+        def round_hid(i):
+            w = CHUNKS[i]
             hid[i] = keep.tile([P, w * PACK], BF16, name="hid%d" % i, align_bytes=64)
+            nc.vector.tensor_tensor(
+                hid[i][:].rearrange("p (c i t) -> p c t i", i=4, t=PACK),
+                fall[i][:].rearrange("p t (c i) -> p c t i", i=4),
+                minus_unit[:].unsqueeze(1).unsqueeze(3).to_broadcast([P, w // 4, PACK, 4]),
+                ALU.mult,
+            )
 
         def product(i):
             j0, w = starts[i], CHUNKS[i]
@@ -230,8 +216,8 @@ def tile_picked_ybitonc_hard_po_kernel(
             rounded[i] = keep.tile([P, w * PACK], BF16, name="rounded%d" % i, align_bytes=64)
             final = i == count - 1
             for b in range(w // P):
-                acc = psum.tile([P, PACK, P], F32, name="out_acc%d" % (j0 // P + b))
-                other = psum.tile([P, PACK, P], F32, name="other", tag="bank0") if final else acc
+                acc = psum.tile([P, PACK, P], F32, name="out_acc", tag=OUT_BANKS[j0 // P + b])
+                other = psum.tile([P, PACK, P], F32, name="other", tag=OUT_BANKS[-1]) if final else acc
                 for t in range(PACK):
                     nc.tensor.matmul_mx(
                         out=(acc if t < 2 else other)[:, t, :],
@@ -266,18 +252,18 @@ def tile_picked_ybitonc_hard_po_kernel(
 
         look_up(0)
         for i in range(count):
-            upper(i, 0, 3)
+            upper(i, 0)
             if i >= 1:
                 product(i - 1)
-            upper(i, 3, PACK)
-            lower(i)
+            for t in range(1, PACK):
+                upper(i, t)
+                lower(i, t - 1)
+            lower(i, PACK - 1)
             if starts[i] + CHUNKS[i] == HALF:
-                look_up(HALF)
-            for t in range(PACK):
-                scale(i, t)
+                look_up(1)
             if i >= 2:
                 planes(i - 2)
-            weave(i)
+            round_hid(i)
         product(count - 1)
         planes(count - 2)
         planes(count - 1)

@@ -21,7 +21,7 @@ PACK = 4
 HALF = S // 2
 SPARE = 16
 CHUNKS = (256, 128, 128)
-LO_ON_SCALAR = {(i, t) for i in range(2) for t in range(3)}
+LO_ON_SCALAR = {(i, t) for i in range(2) for t in range(4)} - {(0, 3)}
 OUT_BANKS = ("out0", "out1", "out2", "bank0_0", "bank0_256")
 
 
@@ -79,8 +79,8 @@ def tile_picked_ybitonc_hard_po_kernel(
         load_scale_rows((nc.scalar, nc.sync, nc.sync, nc.sync), w1_raw_scales, w1_scales[0])
         nc.sync.dma_start(c1_sb[:], c1)
         dir_rows = dir_.rearrange("(p t) j -> p t j", t=PACK)
-        load_scale_rows((nc.sync,) * 4, w2_raw_scales, w2_scales[0])
         nc.sync.dma_start(out=w2_raw[:].bitcast(I32), in_=w2_words[0].bitcast(I32))
+        load_scale_rows((nc.sync,) * 4, w2_raw_scales, w2_scales[0])
         for h in range(2):
             nc.sync.dma_start(out=dir_sb[h][:], in_=dir_rows[:, 2 * h : 2 * h + 2, :])
         nc.sync.dma_start(c2_sb[:], c2)
@@ -129,7 +129,10 @@ def tile_picked_ybitonc_hard_po_kernel(
                     start=True,
                     stop=True,
                 )
-                nc.scalar.copy(y[t][:, cols], acc[:])
+                if t == 0 and j0 == HALF and True:
+                    nc.vector.tensor_copy(y[t][:, cols], acc[:])
+                else:
+                    nc.scalar.copy(y[t][:, cols], acc[:])
             if t >= 1:
                 nc.scalar.activation(yp[t], y_wide[t][:].indirect(c1_sb[:]), ACT.Copy)
                 return
@@ -173,7 +176,7 @@ def tile_picked_ybitonc_hard_po_kernel(
         starts = [sum(CHUNKS[:i]) for i in range(count)]
         mp, lp, up, fall, hid, rounded = {}, {}, {}, {}, {}, {}
 
-        scratch = [diff[2], diff[3], yp[3], gap[2]]
+        scratch = [diff[2], diff[3], yp[3], lift[3]]
 
         def look_up(half):
             picks = entries(c2_sb, half * HALF, HALF)
@@ -183,12 +186,12 @@ def tile_picked_ybitonc_hard_po_kernel(
                     nc.scalar.activation(scratch[t][:, HALF:], lo[t].indirect(picks), ACT.Copy)
 
         def upper(i, t):
-            j0, w = starts[i], CHUNKS[i]
+            j0, w = i * HALF, HALF
             up[i, t] = keep.tile([P, w], F32, name="up%d_%d" % (i, t))
             nc.vector.tensor_tensor(up[i, t][:], stg[t][:, j0 : j0 + w], scratch[t][:, j0 % HALF : j0 % HALF + w], ALU.max)
 
         def lower(i, t):
-            j0, w = starts[i], CHUNKS[i]
+            j0, w = i * HALF, HALF
             if t == 0:
                 fall[i] = keep.tile([P, PACK, w], F32, name="fall%d" % i)
             if (j0 // HALF, t) in LO_ON_SCALAR:
@@ -202,10 +205,18 @@ def tile_picked_ybitonc_hard_po_kernel(
             hid[i] = keep.tile([P, w * PACK], BF16, name="hid%d" % i, align_bytes=64)
             nc.vector.tensor_tensor(
                 hid[i][:].rearrange("p (c i t) -> p c t i", i=4, t=PACK),
-                fall[i][:].rearrange("p t (c i) -> p c t i", i=4),
+                fall[starts[i] // HALF][:, :, starts[i] % HALF : starts[i] % HALF + w].rearrange("p t (c i) -> p c t i", i=4),
                 minus_unit[:].unsqueeze(1).unsqueeze(3).to_broadcast([P, w // 4, PACK, 4]),
                 ALU.mult,
             )
+
+        banks = {}
+        halves = [keep.tile([P, HALF * PACK], BF16, name="rounded%d" % h, align_bytes=64) for h in range(2)]
+        for i in range(count):
+            rounded[i] = halves[starts[i] // HALF][:, starts[i] % HALF * PACK : (starts[i] % HALF + CHUNKS[i]) * PACK]
+
+        def round_out(i):
+            nc.vector.tensor_copy(rounded[i][:].rearrange("p (c t) -> p c t", t=PACK), banks[i][:].rearrange("p t c -> p c t"))
 
         def product(i):
             j0, w = starts[i], CHUNKS[i]
@@ -213,8 +224,7 @@ def tile_picked_ybitonc_hard_po_kernel(
             hid_bytes = keep.tile([P, w], U8, name="hid_bytes%d" % i, align_bytes=64)
             nc.vector.quantize_mx(out=hid_codes[:].bitcast(FP8X4), scales=hid_bytes[:], in_=hid[i][:])
             result = keep.tile([P, PACK, w], F32, name="result%d" % i)
-            rounded[i] = keep.tile([P, w * PACK], BF16, name="rounded%d" % i, align_bytes=64)
-            final = i == count - 1
+            final = False
             for b in range(w // P):
                 acc = psum.tile([P, PACK, P], F32, name="out_acc", tag=OUT_BANKS[j0 // P + b])
                 other = psum.tile([P, PACK, P], F32, name="other", tag=OUT_BANKS[-1]) if final else acc
@@ -228,45 +238,58 @@ def tile_picked_ybitonc_hard_po_kernel(
                         start=True,
                         stop=True,
                     )
-                if final:
+                if final and False:
+                    pairs = rounded[i][:].rearrange("p (c t) -> p c t", t=PACK)
+                    nc.vector.tensor_copy(pairs[:, :, :2], acc[:, :2, :].rearrange("p t c -> p c t"))
+                    nc.scalar.copy(result[:, 2:, :], other[:, 2:, :])
+                    nc.vector.tensor_copy(pairs[:, :, 2:], other[:, 2:, :].rearrange("p t c -> p c t"))
+                    nc.scalar.copy(result[:, :2, :], acc[:, :2, :])
+                elif final:
                     nc.scalar.copy(result[:, :2, :], acc[:, :2, :])
                     nc.scalar.copy(result[:, 2:, :], other[:, 2:, :])
                     nc.vector.tensor_copy(
                         rounded[i][:].rearrange("p (c i t) -> p c t i", i=4, t=PACK),
                         result[:].rearrange("p t (c i) -> p c t i", i=4),
                     )
+                elif i >= 1:
+                    banks[i] = acc
+                    if i == 2:
+                        round_out(2)
+                    nc.scalar.copy(result[:], acc[:])
                 else:
                     nc.scalar.copy(
                         rounded[i][:, PACK * P * b : PACK * P * (b + 1)].rearrange("p (c t) -> p c t", t=PACK),
                         acc[:].rearrange("p t c -> p c t"),
                     )
                     nc.scalar.copy(result[:, :, P * b : P * (b + 1)], acc[:])
-            nc.sync.dma_start(out=out_rows[:, :, j0 : j0 + w], in_=result[:])
+            (nc.scalar if i == 2 else nc.sync).dma_start(out=out_rows[:, :, j0 : j0 + w], in_=result[:])
 
         def planes(i):
-            j0, w = starts[i], CHUNKS[i]
+            j0, w = i * HALF, HALF
             nc.vector.quantize_mx(
-                out=out_codes[:, j0 : j0 + w].bitcast(FP8X4), scales=out_bytes[:, j0 : j0 + w], in_=rounded[i][:]
+                out=out_codes[:, j0 : j0 + w].bitcast(FP8X4), scales=out_bytes[:, j0 : j0 + w], in_=halves[i][:]
             )
             nc.sync.dma_start(out=out_words[:, j0 : j0 + w], in_=out_codes[:, j0 : j0 + w].bitcast(I32))
 
         look_up(0)
-        for i in range(count):
-            upper(i, 0)
-            if i >= 1:
-                product(i - 1)
+        for half in range(2):
+            upper(half, 0)
+            if half == 1:
+                product(0)
             for t in range(1, PACK):
-                upper(i, t)
-                lower(i, t - 1)
-            lower(i, PACK - 1)
-            if starts[i] + CHUNKS[i] == HALF:
+                upper(half, t)
+                lower(half, t - 1)
+            lower(half, PACK - 1)
+            if half == 0:
                 look_up(1)
-            if i >= 2:
-                planes(i - 2)
-            round_hid(i)
-        product(count - 1)
-        planes(count - 2)
-        planes(count - 1)
+                round_hid(0)
+        round_hid(1)
+        round_hid(2)
+        product(1)
+        product(2)
+        planes(0)
+        round_out(1)
+        planes(1)
         for q in range(4):
             queue = nc.sync if q % 2 == 0 else nc.scalar
             queue.dma_start(

from contextlib import ExitStack

import concourse.mybir as mybir

K, T, S, N, H = 512, 1024, 512, 512, 512
FLOPS = 2 * K * H * S + 2 * H * N * S

F32 = mybir.dt.float32
BF16 = mybir.dt.bfloat16
I32 = mybir.dt.int32
U32 = mybir.dt.uint32
U16 = mybir.dt.uint16
U8 = mybir.dt.uint8
FP8X4 = mybir.dt.float8_e4m3fn_x4
FP4X4 = mybir.dt.float4_e2m1fn_x4
ALU = mybir.AluOpType
ACT = mybir.ActivationFunctionType

P = 128
PACK = 4
HALF = S // 2
SPARE = 16
CHUNKS = (256, 128, 128)
LO_ON_SCALAR = {(i, t) for i in range(2) for t in range(4)} - {(0, 3)}
OUT_BANKS = ("out0", "out1", "out2", "bank0_0", "bank0_256")


def load_scale_rows(queues, plane, rows):
    for q, queue in enumerate(queues):
        queue.dma_start(out=plane[32 * q : 32 * q + 4, :].bitcast(I32), in_=rows[4 * q : 4 * q + 4, :].bitcast(I32))


def deal_words(nc, words, raw_words, t0, t1):
    nc.vector.tensor_copy(
        out=words[:].bitcast(U16).rearrange("p (t m) -> p t m", t=t1 - t0),
        in_=raw_words[:].bitcast(U16).rearrange("p (m t) -> p t m", t=PACK)[:, t0:t1],
    )


def deal_scales(nc, scales, raw_scales, t0, t1):
    nc.vector.tensor_copy(
        out=scales[:].rearrange("p (t m) -> p t m", t=PACK)[:, t0:t1],
        in_=raw_scales[:].rearrange("p (m t) -> p t m", t=PACK)[:, t0:t1],
    )


def entries(lst, start, count):
    return lst[:, start // 16 : (start + count) // 16]


def tile_picked_ybitonc_hard_po_kernel(
    tc, x_words, x_scales, w1_words, w1_scales, dir_, unit, w2_words, w2_scales, offs, c1, c2, out_0, out_1, out_2
):
    nc = tc.nc
    with ExitStack() as ctx:
        keep = ctx.enter_context(tc.tile_pool(name="keep", bufs=1))
        psum = ctx.enter_context(tc.psum_pool(name="psum", bufs=1))

        offs_sb = keep.tile([P, S // 16], U16, name="offs_sb")
        c1_sb = keep.tile([P, S // 16], U16, name="c1_sb")
        c2_sb = keep.tile([P, S // 16], U16, name="c2_sb")
        x_table = keep.tile([P, T], I32, name="x_table")
        x_table_scales = keep.tile([P, T], U8, name="x_table_scales")
        w1_raw = keep.tile([P, 2 * H], U8, name="w1_raw")
        w1_raw_scales = keep.tile([P, H], U8, name="w1_raw_scales", tag="w1_reused", align_bytes=64)
        w2_raw = keep.tile([P, 2 * N], U8, name="w2_raw")
        w2_raw_scales = keep.tile([P, N], U8, name="w2_raw_scales")
        unit_sb = keep.tile([P, PACK], F32, name="unit_sb")
        dir_sb = [keep.tile([P, 2, S], F32, name="dir_sb%d" % h) for h in range(2)]

        nc.gpsimd.memset(x_table_scales[:].bitcast(I32), 0)
        nc.gpsimd.memset(w1_raw_scales[:].bitcast(I32), 0)
        nc.gpsimd.memset(w2_raw_scales[:].bitcast(I32), 0)

        nc.sync.dma_start(offs_sb[:], offs)
        load_scale_rows((nc.scalar, nc.sync, nc.scalar, nc.sync), x_table_scales, x_scales[0])
        nc.sync.dma_start(out=x_table[:], in_=x_words[0].rearrange("p n t -> p (n t)").bitcast(I32))
        nc.scalar.dma_start(out=w1_raw[:].bitcast(I32), in_=w1_words[0].bitcast(I32))
        load_scale_rows((nc.scalar, nc.sync, nc.sync, nc.sync), w1_raw_scales, w1_scales[0])
        nc.sync.dma_start(c1_sb[:], c1)
        dir_rows = dir_.rearrange("(p t) j -> p t j", t=PACK)
        nc.sync.dma_start(out=w2_raw[:].bitcast(I32), in_=w2_words[0].bitcast(I32))
        load_scale_rows((nc.sync,) * 4, w2_raw_scales, w2_scales[0])
        for h in range(2):
            nc.sync.dma_start(out=dir_sb[h][:], in_=dir_rows[:, 2 * h : 2 * h + 2, :])
        nc.sync.dma_start(c2_sb[:], c2)
        nc.sync.dma_start(out=unit_sb[:], in_=unit.rearrange("(p t) o -> p (t o)", t=PACK))

        x_codes = keep.tile([P, S], U32, name="x_codes", align_bytes=64)
        x_bytes = keep.tile([P, S], U8, name="x_bytes", align_bytes=64)
        w1_first = keep.tile([P, 2 * P], U8, name="w1_first", align_bytes=64)
        w1_dealt_scales = keep.tile([P, H], U8, name="w1_dealt_scales", align_bytes=64)
        w2_dealt = keep.tile([P, 2 * N], U8, name="w2_dealt", align_bytes=64)
        w2_dealt_scales = keep.tile([P, N], U8, name="w2_dealt_scales", align_bytes=64)

        nc.vector.tensor_copy(x_bytes[:], x_table_scales[:].indirect(offs_sb[:]))
        deal_words(nc, w1_first, w1_raw, 0, 1)
        x_window = x_table[:].bitcast(U32)
        nc.vector.tensor_copy(x_codes[:, :HALF], x_window.indirect(entries(offs_sb, 0, HALF)))
        deal_scales(nc, w1_dealt_scales, w1_raw_scales, 0, PACK)
        nc.vector.tensor_copy(x_codes[:, HALF:], x_window.indirect(entries(offs_sb, HALF, HALF)))
        w1_rest = keep.tile([P, 2 * P * (PACK - 1)], U8, name="w1_rest", tag="w1_reused", align_bytes=64)
        deal_words(nc, w1_rest, w1_raw, 1, PACK)
        w1_tiles = [w1_first[:]] + [w1_rest[:, 2 * P * t : 2 * P * (t + 1)] for t in range(PACK - 1)]

        minus_unit = keep.tile([P, PACK], F32, name="minus_unit")
        nc.gpsimd.tensor_scalar(minus_unit[:], unit_sb[:], -1.0, 0.0, ALU.mult, ALU.add)

        def rows(name, count):
            return [keep.tile([P, S], F32, name="%s%d" % (name, t))[:] for t in range(count)]

        yp, lo, stg, diff, gap, lift = (rows(name, PACK) for name in ("yp", "lo", "stg", "diff", "gap", "lift"))
        y_wide = [keep.tile([P, S + SPARE], F32, name="y%d" % t) for t in range(PACK)]
        y = [tile[:, :S] for tile in y_wide]
        for tile in y_wide:
            nc.gpsimd.memset(tile[:, S:], 0.0)

        def front(t):
            width = HALF if t == 0 else S
            for j0 in range(0, S, width):
                cols = slice(j0, j0 + width)
                acc = psum.tile([P, width], F32, name="y_acc", tag="bank%d_%d" % (t, j0))
                nc.tensor.matmul_mx(
                    out=acc[:],
                    lhsT=w1_tiles[t].bitcast(FP4X4),
                    lhsT_scale=w1_dealt_scales[:, P * t : P * (t + 1)],
                    rhs=x_codes[:, cols].bitcast(FP8X4),
                    rhs_scale=x_bytes[:, cols],
                    start=True,
                    stop=True,
                )
                if t == 0 and j0 == HALF and True:
                    nc.vector.tensor_copy(y[t][:, cols], acc[:])
                else:
                    nc.scalar.copy(y[t][:, cols], acc[:])
            if t >= 1:
                nc.scalar.activation(yp[t], y_wide[t][:].indirect(c1_sb[:]), ACT.Copy)
                return
            for j0 in (0, HALF):
                partners = y_wide[t][:].indirect(entries(c1_sb, j0, HALF))
                if (t, j0) in {(0, 0), (0, HALF)}:
                    nc.vector.tensor_copy(yp[t][:, j0 : j0 + HALF], partners)
                else:
                    nc.scalar.activation(yp[t][:, j0 : j0 + HALF], partners, ACT.Copy)

        def middle(t):
            nc.vector.tensor_tensor(diff[t], yp[t], y[t], ALU.subtract)
            nc.vector.tensor_tensor(lo[t], yp[t], y[t], ALU.min)
            nc.scalar.activation(gap[t], diff[t], ACT.Abs)

        def back(t):
            nc.vector.scalar_tensor_tensor(lift[t], dir_sb[t // 2][:, t % 2, :], 1.0, gap[t], ALU.subtract, ALU.mult)

        def last(t):
            nc.vector.tensor_tensor(stg[t], lo[t], lift[t], ALU.subtract)

        for step in range(PACK + 2):
            if step < PACK:
                front(step)
            if 0 <= step - 2 < PACK:
                back(step - 2)
            if 0 <= step - 1 < PACK:
                middle(step - 1)
            if 0 <= step - 2 < PACK:
                last(step - 2)
            if step == 1:
                deal_words(nc, w2_dealt, w2_raw, 0, PACK)
                deal_scales(nc, w2_dealt_scales, w2_raw_scales, 0, PACK)

        out_codes = keep.tile([P, S], U32, name="out_codes", align_bytes=64)
        out_bytes = keep.tile([P, S], U8, name="out_bytes", align_bytes=64)
        out_rows = out_0.rearrange("(p t) j -> p t j", t=PACK)
        out_words = out_1[0].rearrange("p n t -> p (n t)").bitcast(I32)

        count = len(CHUNKS)
        starts = [sum(CHUNKS[:i]) for i in range(count)]
        mp, lp, up, fall, hid, rounded = {}, {}, {}, {}, {}, {}

        scratch = [diff[2], diff[3], yp[3], lift[3]]

        def look_up(half):
            picks = entries(c2_sb, half * HALF, HALF)
            for t in range(PACK):
                nc.scalar.activation(scratch[t][:, :HALF], stg[t].indirect(picks), ACT.Copy)
                if (half, t) in LO_ON_SCALAR:
                    nc.scalar.activation(scratch[t][:, HALF:], lo[t].indirect(picks), ACT.Copy)

        def upper(i, t):
            j0, w = i * HALF, HALF
            up[i, t] = keep.tile([P, w], F32, name="up%d_%d" % (i, t))
            nc.vector.tensor_tensor(up[i, t][:], stg[t][:, j0 : j0 + w], scratch[t][:, j0 % HALF : j0 % HALF + w], ALU.max)

        def lower(i, t):
            j0, w = i * HALF, HALF
            if t == 0:
                fall[i] = keep.tile([P, PACK, w], F32, name="fall%d" % i)
            if (j0 // HALF, t) in LO_ON_SCALAR:
                partner_lo = scratch[t][:, HALF + j0 % HALF : HALF + j0 % HALF + w]
            else:
                partner_lo = lo[t].indirect(entries(c2_sb, j0, w))
            nc.vector.tensor_tensor(fall[i][:, t, :], partner_lo, up[i, t][:], ALU.subtract)

        def round_hid(i):
            w = CHUNKS[i]
            hid[i] = keep.tile([P, w * PACK], BF16, name="hid%d" % i, align_bytes=64)
            nc.vector.tensor_tensor(
                hid[i][:].rearrange("p (c i t) -> p c t i", i=4, t=PACK),
                fall[starts[i] // HALF][:, :, starts[i] % HALF : starts[i] % HALF + w].rearrange("p t (c i) -> p c t i", i=4),
                minus_unit[:].unsqueeze(1).unsqueeze(3).to_broadcast([P, w // 4, PACK, 4]),
                ALU.mult,
            )

        banks = {}
        halves = [keep.tile([P, HALF * PACK], BF16, name="rounded%d" % h, align_bytes=64) for h in range(2)]
        for i in range(count):
            rounded[i] = halves[starts[i] // HALF][:, starts[i] % HALF * PACK : (starts[i] % HALF + CHUNKS[i]) * PACK]

        def round_out(i):
            nc.vector.tensor_copy(rounded[i][:].rearrange("p (c t) -> p c t", t=PACK), banks[i][:].rearrange("p t c -> p c t"))

        def product(i):
            j0, w = starts[i], CHUNKS[i]
            hid_codes = keep.tile([P, w], U32, name="hid_codes%d" % i, align_bytes=64)
            hid_bytes = keep.tile([P, w], U8, name="hid_bytes%d" % i, align_bytes=64)
            nc.vector.quantize_mx(out=hid_codes[:].bitcast(FP8X4), scales=hid_bytes[:], in_=hid[i][:])
            result = keep.tile([P, PACK, w], F32, name="result%d" % i)
            final = False
            for b in range(w // P):
                acc = psum.tile([P, PACK, P], F32, name="out_acc", tag=OUT_BANKS[j0 // P + b])
                other = psum.tile([P, PACK, P], F32, name="other", tag=OUT_BANKS[-1]) if final else acc
                for t in range(PACK):
                    nc.tensor.matmul_mx(
                        out=(acc if t < 2 else other)[:, t, :],
                        lhsT=w2_dealt[:, 2 * P * t : 2 * P * (t + 1)].bitcast(FP4X4),
                        lhsT_scale=w2_dealt_scales[:, P * t : P * (t + 1)],
                        rhs=hid_codes[:, P * b : P * (b + 1)].bitcast(FP8X4),
                        rhs_scale=hid_bytes[:, P * b : P * (b + 1)],
                        start=True,
                        stop=True,
                    )
                if final and False:
                    pairs = rounded[i][:].rearrange("p (c t) -> p c t", t=PACK)
                    nc.vector.tensor_copy(pairs[:, :, :2], acc[:, :2, :].rearrange("p t c -> p c t"))
                    nc.scalar.copy(result[:, 2:, :], other[:, 2:, :])
                    nc.vector.tensor_copy(pairs[:, :, 2:], other[:, 2:, :].rearrange("p t c -> p c t"))
                    nc.scalar.copy(result[:, :2, :], acc[:, :2, :])
                elif final:
                    nc.scalar.copy(result[:, :2, :], acc[:, :2, :])
                    nc.scalar.copy(result[:, 2:, :], other[:, 2:, :])
                    nc.vector.tensor_copy(
                        rounded[i][:].rearrange("p (c i t) -> p c t i", i=4, t=PACK),
                        result[:].rearrange("p t (c i) -> p c t i", i=4),
                    )
                elif i >= 1:
                    banks[i] = acc
                    if i == 2:
                        round_out(2)
                    nc.scalar.copy(result[:], acc[:])
                else:
                    nc.scalar.copy(
                        rounded[i][:, PACK * P * b : PACK * P * (b + 1)].rearrange("p (c t) -> p c t", t=PACK),
                        acc[:].rearrange("p t c -> p c t"),
                    )
                    nc.scalar.copy(result[:, :, P * b : P * (b + 1)], acc[:])
            (nc.scalar if i == 2 else nc.sync).dma_start(out=out_rows[:, :, j0 : j0 + w], in_=result[:])

        def planes(i):
            j0, w = i * HALF, HALF
            nc.vector.quantize_mx(
                out=out_codes[:, j0 : j0 + w].bitcast(FP8X4), scales=out_bytes[:, j0 : j0 + w], in_=halves[i][:]
            )
            nc.sync.dma_start(out=out_words[:, j0 : j0 + w], in_=out_codes[:, j0 : j0 + w].bitcast(I32))

        look_up(0)
        for half in range(2):
            upper(half, 0)
            if half == 1:
                product(0)
            for t in range(1, PACK):
                upper(half, t)
                lower(half, t - 1)
            lower(half, PACK - 1)
            if half == 0:
                look_up(1)
                round_hid(0)
        round_hid(1)
        round_hid(2)
        product(1)
        product(2)
        planes(0)
        round_out(1)
        planes(1)
        for q in range(4):
            queue = nc.sync if q % 2 == 0 else nc.scalar
            queue.dma_start(
                out=out_2[0, 4 * q : 4 * q + 4, :].bitcast(I32), in_=out_bytes[32 * q : 32 * q + 4, :].bitcast(I32)
            )
